import numpy as np
import ml_dtypes


def mxq(x, axis, fmt="e4m3"):
    dtype, down = {"e4m3": (ml_dtypes.float8_e4m3fn, 7), "e5m2": (ml_dtypes.float8_e5m2, 14)}[fmt]
    v = np.moveaxis(np.asarray(x, np.float32).astype(ml_dtypes.bfloat16).astype(np.float64), axis, -1)
    blocks = v.reshape(v.shape[:-1] + (-1, 32))
    amax = np.abs(blocks).max(-1, keepdims=True)
    byte = np.maximum(np.where(amax > 0, np.frexp(amax)[1] - 1 + 127, 0) - down, 1)
    scale = np.exp2(byte - 127.0)
    codes = (blocks / scale).astype(np.float32).astype(dtype).astype(np.float64)
    return np.moveaxis((codes * scale).reshape(v.shape), -1, axis)


WIDE = False


def mx_kscale(k):
    if not WIDE:
        return np.ones(k)
    levels = np.array([10, -10, 5, -5, 0])
    if k % 512:
        return np.exp2(np.random.permutation(np.resize(levels, k // 32))).repeat(32)
    a = np.empty((k // 512, 16))
    for p in range(k // 512):
        a[p, :8] = np.random.permutation(np.resize(levels, 8))
        for g in range(8):
            far = levels[np.abs(levels - a[p, g]) >= 10]
            a[p, g + 8] = far[np.random.randint(len(far))]
    return np.exp2(a.ravel()).repeat(32)


def f64(x):
    return np.asarray(x).astype(np.float64)


def striped(idx):
    return np.tile(idx.reshape(-1, 16).T, (8, 1)).astype(np.uint16)


def unstriped(offs):
    return offs[:16].T.reshape(-1).astype(np.int64)


def striped8(idx):
    return np.concatenate([x.reshape(-1, 16).T for x in idx]).astype(np.uint16)


def runs(offs, k):
    lists = np.stack([offs[16 * r : 16 * r + 16].T.reshape(-1) for r in range(8)]).astype(np.int64)
    return lists[np.arange(k) % 512 // 64]


def pack_weight(w):
    k, n = w.shape
    w = f64(np.asarray(w, np.float32).astype(ml_dtypes.bfloat16)).reshape(k // 32, 32, n)
    amax = np.abs(w).max(1)
    byte = np.clip(np.where(amax > 0, np.frexp(amax)[1] - 1 + 127 - 7, 1), 1, 254)
    scaled = (w * np.exp2(127.0 - byte)[:, None, :]).reshape(k, n).astype(np.float32)
    words = np.ascontiguousarray(scaled.reshape(k // 512, 128, 4, n).transpose(0, 1, 3, 2)).astype(ml_dtypes.float8_e4m3fn).view(np.uint8)
    return words, np.ascontiguousarray(byte.astype(np.uint8).reshape(k // 512, 16, n))


def unpack_weight(words, scales):
    g, p, n, _ = words.shape
    vals = np.ascontiguousarray(words).view(ml_dtypes.float8_e4m3fn).astype(np.float64) * np.repeat(np.exp2(scales.astype(np.float64) - 127.0), 8, axis=1)[..., None]
    return vals.transpose(0, 1, 3, 2).reshape(g * 512, n)


E2M1 = np.array([0.0, 0.5, 1.0, 1.5, 2.0, 3.0, 4.0, 6.0, -0.0, -0.5, -1.0, -1.5, -2.0, -3.0, -4.0, -6.0])


def pack_fp4(w):
    k, n = w.shape
    w = f64(np.asarray(w, np.float32).astype(ml_dtypes.bfloat16)).reshape(k // 32, 32, n)
    amax = np.abs(w).max(1)
    mant, ex = np.frexp(amax / 6.0)
    byte = np.clip(np.where(amax > 0, np.where(mant > 0.5, ex, ex - 1) + 127, 1), 1, 254)
    scaled = (w * np.exp2(127.0 - byte)[:, None, :]).reshape(k, n).astype(np.float32)
    c = np.ascontiguousarray(scaled.reshape(k // 512, 128, 4, n).transpose(0, 1, 3, 2)).astype(ml_dtypes.float4_e2m1fn).view(np.uint8) & 0xF
    words = (c[..., 0::2] | (c[..., 1::2] << 4)).reshape(k // 512, 128, 2 * n)
    return np.ascontiguousarray(words), np.ascontiguousarray(byte.astype(np.uint8).reshape(k // 512, 16, n))


def unpack_fp4(words, scales):
    g, _, n = scales.shape
    words = np.ascontiguousarray(words).reshape(g, 128, n, 2)
    nib = np.empty((g, 128, n, 4), np.uint8)
    nib[..., 0::2] = words & 0xF
    nib[..., 1::2] = words >> 4
    vals = E2M1[nib] * np.repeat(np.exp2(scales.astype(np.float64) - 127.0), 8, axis=1)[..., None]
    return vals.transpose(0, 1, 3, 2).reshape(g * 512, n)


def planes(y):
    n, m = y.shape
    v = y.astype(np.float32).astype(ml_dtypes.bfloat16).astype(np.float64).reshape(n // 32, 32, m)
    top = np.abs(v).max(1)
    byte = np.clip(np.where(top > 0, np.frexp(top)[1] - 1 + 127 - 7, 1), 1, 254)
    codes = (v * np.exp2(127.0 - byte)[:, None, :]).reshape(n, m).astype(np.float32).astype(ml_dtypes.float8_e4m3fn).view(np.uint8)
    words = codes.reshape(n // 512, 128, 4, m).transpose(0, 1, 3, 2)
    return np.ascontiguousarray(words), np.ascontiguousarray(byte.astype(np.uint8).reshape(n // 512, 16, m))


K, T, S, N, H, W = 512, 2048, 512, 512, 512, 2048


def setup_inputs():
    n = np.random.standard_normal
    s = mx_kscale(K)[:, None]
    u = mx_kscale(H)
    packed_xT = pack_weight(n((K, T)) * s)
    packed_w1 = pack_fp4(n((K, H)) / np.sqrt(K) / s)
    packed_w2 = pack_fp4(n((H, N)) / np.sqrt(H) / u[:, None])
    return {
        "x_words": packed_xT[0],
        "x_scales": packed_xT[1],
        "w1_words": packed_w1[0],
        "w1_scales": packed_w1[1],
        "gn": (np.random.uniform(0.5, 1.5, (H, 1)) * u[:, None]).astype(np.float32),
        "w2_words": packed_w2[0],
        "w2_scales": packed_w2[1],
        "offs": striped(np.random.permutation(T)[:S]),
        "n1": striped(np.random.randint(0, S, W)),
        "n2": striped8(np.stack([np.random.permutation(S) for _ in range(8)])),
        "n3": striped8(np.stack([np.random.permutation(S) for _ in range(8)])),
    }


def reference(x_words, x_scales, w1_words, w1_scales, gn, w2_words, w2_scales, offs, n1, n2, n3):
    xq = unpack_weight(x_words, x_scales)[:, unstriped(offs)]
    y = unpack_fp4(w1_words, w1_scales).T @ xq
    mb = y[:, unstriped(n1)]
    mn = mb.reshape(H, S, 4).min(axis=2)
    mx = mb.reshape(H, S, 4).max(axis=2)
    z = f64(gn) * (np.maximum(y, mn) - (0.5 * mx))
    h = unpack_fp4(w2_words, w2_scales).T @ mxq(z, 0, "e4m3")
    out_0 = h * (np.tanh(y[np.arange(H)[:, None], runs(n2, H)] - (y[np.arange(H)[:, None], runs(n3, H)])))
    return (out_0,) + planes(out_0)

@@ -1,0 +1,302 @@
+from contextlib import ExitStack
+
+import concourse.mybir as mybir
+
+K, T, S, N, H, W = 512, 2048, 512, 512, 512, 2048
+FLOPS = 2 * K * H * S + 2 * H * N * S
+
+F32 = mybir.dt.float32
+BF16 = mybir.dt.bfloat16
+I32 = mybir.dt.int32
+U32 = mybir.dt.uint32
+U16 = mybir.dt.uint16
+U8 = mybir.dt.uint8
+FP8X4 = mybir.dt.float8_e4m3fn_x4
+FP4X4 = mybir.dt.float4_e2m1fn_x4
+ALU = mybir.AluOpType
+ACT = mybir.ActivationFunctionType
+
+P = 128
+PACK = 4
+HALF = 256
+CHUNK = 128
+CHUNKS = S // CHUNK
+MEMBERS = 4
+WINDOW = 1024
+WIDE = 256
+RING = 3
+
+
+def tile_picked_skipjointbgmid_none_po_kernel(
+    tc, x_words, x_scales, w1_words, w1_scales, gn, w2_words, w2_scales, offs, n1, n2, n3, out_0, out_1, out_2
+):
+    nc = tc.nc
+    with ExitStack() as ctx:
+        keep = ctx.enter_context(tc.tile_pool(name="keep", bufs=1))
+        ring = ctx.enter_context(tc.tile_pool(name="ring", bufs=RING))
+        work = ctx.enter_context(tc.tile_pool(name="work", bufs=2))
+        ybanks = ctx.enter_context(tc.psum_pool(name="ybanks", bufs=1))
+        hbanks = ctx.enter_context(tc.psum_pool(name="hbanks", bufs=1))
+
+        offs_sb = keep.tile([P, S // 16], U16, name="offs_sb")
+        n1_sb = keep.tile([P, W // 16], U16, name="n1_sb")
+        n2_sb = keep.tile([P, S // 16], U16, name="n2_sb")
+        n3_sb = keep.tile([P, S // 16], U16, name="n3_sb")
+        x_table = keep.tile([P, T], I32, name="x_table", align_bytes=64)
+        x_bytes = keep.tile([P, T], U8, name="x_bytes", tag="x_bytes", align_bytes=64)
+        w_raw = keep.tile([P, 2 * H], U8, name="w_raw", align_bytes=64)
+        ws_raw = keep.tile([P, H], U8, name="ws_raw", align_bytes=64)
+
+        def load_scale_rows(queues, tile, rows):
+            for q, queue in enumerate(queues):
+                queue.dma_start(
+                    out=tile[32 * q : 32 * q + 4, :].bitcast(I32), in_=rows[0, 4 * q : 4 * q + 4, :].bitcast(I32)
+                )
+
+        nc.vector.memset(x_bytes[:].bitcast(I32), 0)
+        nc.gpsimd.memset(ws_raw[:].bitcast(I32), 0)
+        y_rows = [keep.tile([P, WINDOW], F32, name=f"y_rows{t}") for t in range(PACK)]
+        for t in range(PACK):
+            nc.vector.memset(y_rows[t][:, S:], 0.0)
+        nc.sync.dma_start(out=offs_sb[:], in_=offs)
+        nc.scalar.dma_start(out=w_raw[:].bitcast(I32), in_=w1_words[0].bitcast(I32))
+        nc.sync.dma_start(out=n1_sb[:], in_=n1)
+        nc.sync.dma_start(out=n2_sb[:], in_=n2)
+        nc.sync.dma_start(out=n3_sb[:], in_=n3)
+        nc.sync.dma_start(out=x_table[:], in_=x_words[0].rearrange("p c r -> p (c r)").bitcast(I32))
+        load_scale_rows([nc.sync] * 4, x_bytes, x_scales)
+        load_scale_rows([nc.scalar, nc.scalar, nc.scalar, nc.gpsimd], ws_raw, w1_scales)
+
+        def deal_words(codes):
+            nc.vector.tensor_copy(
+                out=codes[:].rearrange("p t (m b) -> p t m b", b=2),
+                in_=w_raw[:].rearrange("p (m t b) -> p t m b", t=PACK, b=2),
+            )
+
+        def deal_scales(engine, plane, ts):
+            engine.tensor_copy(out=plane[:, ts, :], in_=ws_raw[:].rearrange("p (m t) -> p t m", t=PACK)[:, ts, :])
+
+        w1_codes = keep.tile([P, PACK, 2 * P], U8, name="w1_codes", align_bytes=64)
+        w1_plane = keep.tile([P, PACK, P], U8, name="w1_plane", align_bytes=64)
+        w2_codes = keep.tile([P, PACK, 2 * P], U8, name="w2_codes", align_bytes=64)
+        w2_plane = keep.tile([P, PACK, P], U8, name="w2_plane", align_bytes=64)
+        x_codes = keep.tile([P, S], U32, name="x_codes", align_bytes=64)
+        x_plane = keep.tile([P, S], U8, name="x_plane", align_bytes=64)
+
+        deal_words(w1_codes)
+        deal_scales(nc.gpsimd, w1_plane, slice(0, 2))
+        deal_scales(nc.gpsimd, w1_plane, slice(2, 4))
+        nc.vector.tensor_copy(out=x_plane[:], in_=x_bytes[:].indirect(offs_sb[:]))
+        for half in range(2):
+            cols = slice(half * HALF, (half + 1) * HALF)
+            nc.vector.tensor_copy(
+                out=x_codes[:, cols],
+                in_=x_table[:].bitcast(U32).indirect(offs_sb[:, half * HALF // 16 : (half + 1) * HALF // 16]),
+            )
+
+        nc.sync.dma_start(out=w_raw[:].bitcast(I32), in_=w2_words[0].bitcast(I32))
+        load_scale_rows([nc.sync] * 4, ws_raw, w2_scales)
+        gain = keep.tile([P, PACK], F32, name="gain", tag="x_bytes", align_bytes=64)
+        nc.sync.dma_start(out=gain[:], in_=gn.rearrange("(p t) o -> p (t o)", t=PACK))
+
+        y_bank = {}
+        for pair in range(2):
+            for half in range(2):
+                cols = slice(half * HALF, (half + 1) * HALF)
+                bank = ybanks.tile([P, 2, HALF], F32, name=f"y_bank{pair}{half}")
+                y_bank[pair, half] = bank
+                for e in range(2):
+                    t = 2 * pair + e
+                    nc.tensor.matmul_mx(
+                        out=bank[:, e, :],
+                        lhsT=w1_codes[:, t, :].bitcast(FP4X4),
+                        lhsT_scale=w1_plane[:, t, :],
+                        rhs=x_codes[:, cols].bitcast(FP8X4),
+                        rhs_scale=x_plane[:, cols],
+                        start=True,
+                        stop=True,
+                    )
+        for t in range(PACK):
+            for half in range(2):
+                cols = slice(half * HALF, (half + 1) * HALF)
+                src = y_bank[t // 2, half][:, t % 2, :]
+                if t == 0:
+                    nc.scalar.copy(out=y_rows[t][:, cols], in_=src)
+                else:
+                    nc.vector.tensor_copy(out=y_rows[t][:, cols], in_=src)
+
+        z_codes = keep.tile([P, S], U32, name="z_codes", align_bytes=64)
+        z_plane = keep.tile([P, S], U8, name="z_plane", align_bytes=64)
+        o_codes = keep.tile([P, S], I32, name="o_codes", align_bytes=64)
+        o_plane = keep.tile([P, S], U8, name="o_plane", align_bytes=64)
+        out_rows = out_0.rearrange("(p t) j -> p t j", t=PACK)
+        out_words = out_1[0].rearrange("p c r -> p (c r)").bitcast(I32)
+
+        members, lows, highs, ups, diffs, zs, ends, gates, results, roundeds, h_bank = ({} for k in range(11))
+
+        def fetch_members(c, pair):
+            tile = keep.tile([P, 2, CHUNK * MEMBERS], F32, name=f"members{c}{pair}")
+            members[c, pair] = tile[:].rearrange("p e (j i) -> p j e i", i=MEMBERS)
+            entries = slice(c * CHUNK * MEMBERS // 16, (c + 1) * CHUNK * MEMBERS // 16)
+            for e in range(2):
+                nc.scalar.activation(tile[:, e, :], y_rows[2 * pair + e][:].indirect(n1_sb[:, entries]), ACT.Copy)
+
+        def pair_low(c, pair):
+            m = members[c, pair]
+            lows[c, pair] = work.tile([P, CHUNK, 2, 2], F32, name="low")
+            nc.vector.tensor_tensor(lows[c, pair][:], m[:, :, :, 0:2], m[:, :, :, 2:4], ALU.min)
+
+        def extremes(c, pair):
+            m, lo = members[c, pair], lows[c, pair]
+            hi = work.tile([P, CHUNK, 2, 2], F32, name="hi")
+            nc.vector.tensor_tensor(hi[:], m[:, :, :, 0:2], m[:, :, :, 2:4], ALU.max)
+            mn = work.tile([P, CHUNK, 2], F32, name="mn")
+            mx = work.tile([P, CHUNK, 2], F32, name="mx")
+            nc.vector.tensor_tensor(mn[:], lo[:, :, :, 0], lo[:, :, :, 1], ALU.min)
+            nc.vector.tensor_tensor(mx[:], hi[:, :, :, 0], hi[:, :, :, 1], ALU.max)
+            half, first = divmod(c * CHUNK, HALF)
+            own = y_bank[pair, half][:, :, first : first + CHUNK].rearrange("p e j -> p j e")
+            up = work.tile([P, CHUNK, 2], F32, name="up")
+            nc.vector.tensor_tensor(up[:], own, mn[:], ALU.max)
+            highs[c, pair], ups[c, pair] = mx, up
+
+        def difference(c, pair):
+            if pair == 0:
+                diffs[c] = work.tile([P, 2, CHUNK, 2], F32, name="diff")
+            nc.vector.scalar_tensor_tensor(
+                diffs[c][:, pair, :, :].rearrange("p j e -> p (j e)"),
+                highs[c, pair][:].rearrange("p j e -> p (j e)"),
+                -0.5,
+                ups[c, pair][:].rearrange("p j e -> p (j e)"),
+                ALU.mult,
+                ALU.add,
+            )
+
+        def scale_round(c):
+            zs[c] = work.tile([P, CHUNK, 2, 2], BF16, name="z", align_bytes=64)
+            g = gain[:].rearrange("p (a e) -> p a e", e=2).unsqueeze(1).to_broadcast([P, CHUNK, 2, 2])
+            nc.vector.tensor_tensor(zs[c][:], diffs[c][:].rearrange("p a j e -> p j a e"), g, ALU.mult)
+
+        def second_product(c):
+            cols = slice(c * CHUNK, (c + 1) * CHUNK)
+            nc.vector.quantize_mx(
+                out=z_codes[:, cols].bitcast(FP8X4),
+                scales=z_plane[:, cols],
+                in_=zs[c][:].rearrange("p j a e -> p (j a e)"),
+            )
+            wide, first = divmod(c * CHUNK, WIDE)
+            for t in range(PACK):
+                if (wide, t // 2) not in h_bank:
+                    h_bank[wide, t // 2] = hbanks.tile([P, 2, WIDE], F32, name=f"h_bank{wide}{t // 2}")
+                nc.tensor.matmul_mx(
+                    out=h_bank[wide, t // 2][:, t % 2, first : first + CHUNK],
+                    lhsT=w2_codes[:, t, :].bitcast(FP4X4),
+                    lhsT_scale=w2_plane[:, t, :],
+                    rhs=z_codes[:, cols].bitcast(FP8X4),
+                    rhs_scale=z_plane[:, cols],
+                    start=True,
+                    stop=True,
+                )
+
+        def fetch_ends(wide, pair):
+            tile = ring.tile([P, 2, 2 * WIDE], F32, name="ends")
+            ends[wide, pair] = tile
+            entries = slice(wide * WIDE // 16, (wide + 1) * WIDE // 16)
+            for e in range(2):
+                for side, places in enumerate((n2_sb, n3_sb)):
+                    nc.scalar.activation(
+                        tile[:, side, e * WIDE : (e + 1) * WIDE],
+                        y_rows[2 * pair + e][:].indirect(places[:, entries]),
+                        ACT.Copy,
+                    )
+
+        def subtract(wide, pair, cols=slice(0, 2 * WIDE)):
+            tile = ends[wide, pair]
+            nc.vector.tensor_tensor(tile[:, 0, cols], tile[:, 0, cols], tile[:, 1, cols], ALU.subtract)
+
+        def gate(wide, pair, cols=slice(0, 2 * WIDE)):
+            if (wide, pair) not in gates:
+                gates[wide, pair] = keep.tile([P, 2 * WIDE], F32, name=f"gate{wide}{pair}")
+            nc.scalar.activation(gates[wide, pair][:, cols], ends[wide, pair][:, 0, cols], ACT.Tanh)
+
+        def multiply(wide, pair, cols=slice(0, 2 * WIDE)):
+            if wide not in results:
+                results[wide] = work.tile([P, 2, 2 * WIDE], F32, name="result")
+            res = results[wide]
+            nc.vector.tensor_tensor(
+                res[:, pair, cols],
+                h_bank[wide, pair][:].rearrange("p e j -> p (e j)")[:, cols],
+                gates[wide, pair][:, cols],
+                ALU.mult,
+            )
+
+        def store(wide, ts):
+            res = results[wide][:].rearrange("p a (e j) -> p (a e) j", e=2)
+            nc.sync.dma_start(out=out_rows[:, ts, wide * WIDE : (wide + 1) * WIDE], in_=res[:, ts, :])
+
+        def round_result(wide):
+            roundeds[wide] = work.tile([P, WIDE, PACK], BF16, name="rounded", align_bytes=64)
+            nc.vector.tensor_copy(
+                out=roundeds[wide][:].rearrange("p (c i) t -> p c t i", i=4),
+                in_=results[wide][:].rearrange("p a (e c i) -> p c (a e) i", e=2, i=4),
+            )
+
+        def planes(wide):
+            cols = slice(wide * WIDE, (wide + 1) * WIDE)
+            nc.vector.quantize_mx(
+                out=o_codes[:, cols].bitcast(FP8X4),
+                scales=o_plane[:, cols],
+                in_=roundeds[wide][:].rearrange("p j t -> p (j t)"),
+            )
+            nc.sync.dma_start(out=out_words[:, cols], in_=o_codes[:, cols])
+
+        deal_words(w2_codes)
+        deal_scales(nc.vector, w2_plane, slice(0, 4))
+        units = [(c, pair) for c in range(CHUNKS) for pair in range(2)]
+        for k, (c, pair) in enumerate(units):
+            fetch_members(c, pair)
+            pair_low(c, pair)
+            if k > 0:
+                difference(*units[k - 1])
+            if pair == 1 and c > 0:
+                second_product(c - 1)
+            extremes(c, pair)
+            if pair == 0 and c > 0:
+                scale_round(c - 1)
+
+        last = CHUNKS - 1
+        left, right = slice(0, WIDE), slice(WIDE, 2 * WIDE)
+        fetch_ends(0, 0)
+        fetch_ends(0, 1)
+        fetch_ends(1, 0)
+        subtract(0, 0)
+        gate(0, 0)
+        difference(last, 1)
+        subtract(0, 1)
+        scale_round(last)
+        fetch_ends(1, 1)
+        gate(0, 1)
+        subtract(1, 0)
+        second_product(last)
+        multiply(0, 0)
+        gate(1, 0)
+        multiply(0, 1)
+        store(0, slice(0, 4))
+        subtract(1, 1, left)
+        round_result(0)
+        subtract(1, 1, right)
+        gate(1, 1, left)
+        gate(1, 1, right)
+        multiply(1, 0)
+        store(1, slice(0, 2))
+        planes(0)
+        multiply(1, 1, left)
+        multiply(1, 1, right)
+        store(1, slice(2, 4))
+        round_result(1)
+        planes(1)
+
+        for q in range(4):
+            nc.scalar.dma_start(
+                out=out_2[0, 4 * q : 4 * q + 4, :].bitcast(I32), in_=o_plane[32 * q : 32 * q + 4, :].bitcast(I32)
+            )

@@ -1,6 +1,7 @@
 from contextlib import ExitStack
 
 import concourse.mybir as mybir
+from concourse.masks import make_identity
 
 K, T, S, N, H, W = 512, 2048, 512, 512, 512, 2048
 FLOPS = 2 * K * H * S + 2 * H * N * S
@@ -19,12 +20,9 @@ ACT = mybir.ActivationFunctionType
 P = 128
 PACK = 4
 HALF = 256
-CHUNK = 128
-CHUNKS = S // CHUNK
+CHUNKS = ((0, 128), (128, 192), (320, 192))
 MEMBERS = 4
 WINDOW = 1024
-WIDE = 256
-RING = 3
 
 
 def tile_picked_skipjointbgmid_none_po_kernel(
@@ -33,16 +31,14 @@ def tile_picked_skipjointbgmid_none_po_kernel(
     nc = tc.nc
     with ExitStack() as ctx:
         keep = ctx.enter_context(tc.tile_pool(name="keep", bufs=1))
-        ring = ctx.enter_context(tc.tile_pool(name="ring", bufs=RING))
         work = ctx.enter_context(tc.tile_pool(name="work", bufs=2))
-        ybanks = ctx.enter_context(tc.psum_pool(name="ybanks", bufs=1))
-        hbanks = ctx.enter_context(tc.psum_pool(name="hbanks", bufs=1))
+        psum = ctx.enter_context(tc.psum_pool(name="psum", bufs=1))
 
         offs_sb = keep.tile([P, S // 16], U16, name="offs_sb")
         n1_sb = keep.tile([P, W // 16], U16, name="n1_sb")
         n2_sb = keep.tile([P, S // 16], U16, name="n2_sb")
         n3_sb = keep.tile([P, S // 16], U16, name="n3_sb")
-        x_table = keep.tile([P, T], I32, name="x_table", align_bytes=64)
+        x_table = keep.tile([P, T], I32, name="x_table", tag="x_table", align_bytes=64)
         x_bytes = keep.tile([P, T], U8, name="x_bytes", tag="x_bytes", align_bytes=64)
         w_raw = keep.tile([P, 2 * H], U8, name="w_raw", align_bytes=64)
         ws_raw = keep.tile([P, H], U8, name="ws_raw", align_bytes=64)
@@ -53,24 +49,26 @@ def tile_picked_skipjointbgmid_none_po_kernel(
                     out=tile[32 * q : 32 * q + 4, :].bitcast(I32), in_=rows[0, 4 * q : 4 * q + 4, :].bitcast(I32)
                 )
 
-        nc.vector.memset(x_bytes[:].bitcast(I32), 0)
+        nc.gpsimd.memset(x_bytes[:].bitcast(I32), 0)
         nc.gpsimd.memset(ws_raw[:].bitcast(I32), 0)
         y_rows = [keep.tile([P, WINDOW], F32, name=f"y_rows{t}") for t in range(PACK)]
         for t in range(PACK):
             nc.vector.memset(y_rows[t][:, S:], 0.0)
         nc.sync.dma_start(out=offs_sb[:], in_=offs)
-        nc.scalar.dma_start(out=w_raw[:].bitcast(I32), in_=w1_words[0].bitcast(I32))
+        nc.sync.dma_start(out=w_raw[:].bitcast(I32), in_=w1_words[0].bitcast(I32))
+        load_scale_rows([nc.sync] * 4, x_bytes, x_scales)
+        nc.sync.dma_start(out=x_table[:], in_=x_words[0].rearrange("p c r -> p (c r)").bitcast(I32))
+        load_scale_rows([nc.sync, nc.sync, nc.sync, nc.gpsimd], ws_raw, w1_scales)
+        ident = keep.tile([P, P], F32, name="ident")
+        make_identity(nc, ident[:])
         nc.sync.dma_start(out=n1_sb[:], in_=n1)
         nc.sync.dma_start(out=n2_sb[:], in_=n2)
         nc.sync.dma_start(out=n3_sb[:], in_=n3)
-        nc.sync.dma_start(out=x_table[:], in_=x_words[0].rearrange("p c r -> p (c r)").bitcast(I32))
-        load_scale_rows([nc.sync] * 4, x_bytes, x_scales)
-        load_scale_rows([nc.scalar, nc.scalar, nc.scalar, nc.gpsimd], ws_raw, w1_scales)
 
-        def deal_words(codes):
+        def deal_words(codes, raw):
             nc.vector.tensor_copy(
                 out=codes[:].rearrange("p t (m b) -> p t m b", b=2),
-                in_=w_raw[:].rearrange("p (m t b) -> p t m b", t=PACK, b=2),
+                in_=raw[:].rearrange("p (m t b) -> p t m b", t=PACK, b=2),
             )
 
         def deal_scales(engine, plane, ts):
@@ -78,52 +76,61 @@ def tile_picked_skipjointbgmid_none_po_kernel(
 
         w1_codes = keep.tile([P, PACK, 2 * P], U8, name="w1_codes", align_bytes=64)
         w1_plane = keep.tile([P, PACK, P], U8, name="w1_plane", align_bytes=64)
-        w2_codes = keep.tile([P, PACK, 2 * P], U8, name="w2_codes", align_bytes=64)
-        w2_plane = keep.tile([P, PACK, P], U8, name="w2_plane", align_bytes=64)
         x_codes = keep.tile([P, S], U32, name="x_codes", align_bytes=64)
         x_plane = keep.tile([P, S], U8, name="x_plane", align_bytes=64)
 
-        deal_words(w1_codes)
+        deal_words(w1_codes, w_raw)
         deal_scales(nc.gpsimd, w1_plane, slice(0, 2))
         deal_scales(nc.gpsimd, w1_plane, slice(2, 4))
         nc.vector.tensor_copy(out=x_plane[:], in_=x_bytes[:].indirect(offs_sb[:]))
         for half in range(2):
-            cols = slice(half * HALF, (half + 1) * HALF)
             nc.vector.tensor_copy(
-                out=x_codes[:, cols],
+                out=x_codes[:, half * HALF : (half + 1) * HALF],
                 in_=x_table[:].bitcast(U32).indirect(offs_sb[:, half * HALF // 16 : (half + 1) * HALF // 16]),
             )
 
-        nc.sync.dma_start(out=w_raw[:].bitcast(I32), in_=w2_words[0].bitcast(I32))
+        w2_raw = keep.tile([P, 2 * N], U8, name="w2_raw", tag="x_table", align_bytes=64)
+        nc.sync.dma_start(out=w2_raw[:].bitcast(I32), in_=w2_words[0].bitcast(I32))
         load_scale_rows([nc.sync] * 4, ws_raw, w2_scales)
-        gain = keep.tile([P, PACK], F32, name="gain", tag="x_bytes", align_bytes=64)
-        nc.sync.dma_start(out=gain[:], in_=gn.rearrange("(p t) o -> p (t o)", t=PACK))
+        gain = keep.tile([P, H], F32, name="gain", tag="x_bytes", align_bytes=64)
+        nc.sync.dma_start(out=gain[:], in_=gn.rearrange("i o -> (i o)").partition_broadcast(P))
 
         y_bank = {}
-        for pair in range(2):
+
+        def first_product(t, half):
+            cols = slice(half * HALF, (half + 1) * HALF)
+            if t % 2 == 0:
+                y_bank[t // 2, half] = psum.tile([P, 2, HALF], F32, name="y_bank", tag=f"bank{2 * half + t // 2}")
+            nc.tensor.matmul_mx(
+                out=y_bank[t // 2, half][:, t % 2, :],
+                lhsT=w1_codes[:, t, :].bitcast(FP4X4),
+                lhsT_scale=w1_plane[:, t, :],
+                rhs=x_codes[:, cols].bitcast(FP8X4),
+                rhs_scale=x_plane[:, cols],
+                start=True,
+                stop=True,
+            )
+
+        def fill_window(t, half):
+            cols = slice(half * HALF, (half + 1) * HALF)
+            src = y_bank[t // 2, half][:, t % 2, :]
+            if t == 0:
+                nc.scalar.activation(y_rows[t][:, cols], src, ACT.Copy, scale=-0.5)
+            else:
+                nc.vector.tensor_scalar(y_rows[t][:, cols], src, -0.5, None, ALU.mult)
+
+        first_product(0, 0)
+        first_product(1, 0)
+        fill_window(0, 0)
+        first_product(0, 1)
+        fill_window(0, 1)
+        first_product(1, 1)
+        for half in range(2):
+            first_product(2, half)
+            first_product(3, half)
+        for t in range(1, PACK):
             for half in range(2):
-                cols = slice(half * HALF, (half + 1) * HALF)
-                bank = ybanks.tile([P, 2, HALF], F32, name=f"y_bank{pair}{half}")
-                y_bank[pair, half] = bank
-                for e in range(2):
-                    t = 2 * pair + e
-                    nc.tensor.matmul_mx(
-                        out=bank[:, e, :],
-                        lhsT=w1_codes[:, t, :].bitcast(FP4X4),
-                        lhsT_scale=w1_plane[:, t, :],
-                        rhs=x_codes[:, cols].bitcast(FP8X4),
-                        rhs_scale=x_plane[:, cols],
-                        start=True,
-                        stop=True,
-                    )
-        for t in range(PACK):
-            for half in range(2):
-                cols = slice(half * HALF, (half + 1) * HALF)
-                src = y_bank[t // 2, half][:, t % 2, :]
-                if t == 0:
-                    nc.scalar.copy(out=y_rows[t][:, cols], in_=src)
-                else:
-                    nc.vector.tensor_copy(out=y_rows[t][:, cols], in_=src)
+                fill_window(t, half)
 
         z_codes = keep.tile([P, S], U32, name="z_codes", align_bytes=64)
         z_plane = keep.tile([P, S], U8, name="z_plane", align_bytes=64)
@@ -131,65 +138,82 @@ def tile_picked_skipjointbgmid_none_po_kernel(
         o_plane = keep.tile([P, S], U8, name="o_plane", align_bytes=64)
         out_rows = out_0.rearrange("(p t) j -> p t j", t=PACK)
         out_words = out_1[0].rearrange("p c r -> p (c r)").bitcast(I32)
+        upper = keep.tile([P, PACK, S], F32, name="upper")
+        lower = keep.tile([P, PACK, S], F32, name="lower")
 
-        members, lows, highs, ups, diffs, zs, ends, gates, results, roundeds, h_bank = ({} for k in range(11))
+        members, sums, turned, z, h_bank = ({} for k in range(5))
 
         def fetch_members(c, pair):
-            tile = keep.tile([P, 2, CHUNK * MEMBERS], F32, name=f"members{c}{pair}")
-            members[c, pair] = tile[:].rearrange("p e (j i) -> p j e i", i=MEMBERS)
-            entries = slice(c * CHUNK * MEMBERS // 16, (c + 1) * CHUNK * MEMBERS // 16)
+            first, width = CHUNKS[c]
+            tile = keep.tile([P, 2, width * MEMBERS], F32, name="members", tag=f"members{c}{pair}", align_bytes=64)
+            members[c, pair] = tile[:].rearrange("p e (j i) -> p (e j) i", i=MEMBERS)
+            entries = slice(first * MEMBERS // 16, (first + width) * MEMBERS // 16)
             for e in range(2):
                 nc.scalar.activation(tile[:, e, :], y_rows[2 * pair + e][:].indirect(n1_sb[:, entries]), ACT.Copy)
 
-        def pair_low(c, pair):
-            m = members[c, pair]
-            lows[c, pair] = work.tile([P, CHUNK, 2, 2], F32, name="low")
-            nc.vector.tensor_tensor(lows[c, pair][:], m[:, :, :, 0:2], m[:, :, :, 2:4], ALU.min)
-
         def extremes(c, pair):
-            m, lo = members[c, pair], lows[c, pair]
-            hi = work.tile([P, CHUNK, 2, 2], F32, name="hi")
-            nc.vector.tensor_tensor(hi[:], m[:, :, :, 0:2], m[:, :, :, 2:4], ALU.max)
-            mn = work.tile([P, CHUNK, 2], F32, name="mn")
-            mx = work.tile([P, CHUNK, 2], F32, name="mx")
-            nc.vector.tensor_tensor(mn[:], lo[:, :, :, 0], lo[:, :, :, 1], ALU.min)
-            nc.vector.tensor_tensor(mx[:], hi[:, :, :, 0], hi[:, :, :, 1], ALU.max)
-            half, first = divmod(c * CHUNK, HALF)
-            own = y_bank[pair, half][:, :, first : first + CHUNK].rearrange("p e j -> p j e")
-            up = work.tile([P, CHUNK, 2], F32, name="up")
-            nc.vector.tensor_tensor(up[:], own, mn[:], ALU.max)
-            highs[c, pair], ups[c, pair] = mx, up
+            m = members[c, pair]
+            first, width = CHUNKS[c]
+            ts = slice(2 * pair, 2 * pair + 2)
+            hi = work.tile([P, 2, width, 2], F32, name="hi")
+            lo = work.tile([P, 2, width, 2], F32, name="lo")
+            nc.vector.tensor_tensor(hi[:].rearrange("p e j i -> p (e j) i"), m[:, :, 0:2], m[:, :, 2:4], ALU.max)
+            nc.vector.tensor_tensor(lo[:].rearrange("p e j i -> p (e j) i"), m[:, :, 0:2], m[:, :, 2:4], ALU.min)
+            top = work.tile([P, 2, width], F32, name="top")
+            nc.vector.tensor_tensor(top[:], hi[:, :, :, 0], hi[:, :, :, 1], ALU.max)
+            nc.vector.tensor_tensor(lower[:, ts, first : first + width], lo[:, :, :, 0], lo[:, :, :, 1], ALU.min)
+            for half in range(2):
+                a, b = max(first, half * HALF), min(first + width, (half + 1) * HALF)
+                if a < b:
+                    nc.vector.scalar_tensor_tensor(
+                        upper[:, ts, a:b],
+                        top[:, :, a - first : b - first],
+                        -2.0,
+                        y_bank[pair, half][:, :, a - half * HALF : b - half * HALF],
+                        ALU.mult,
+                        ALU.max,
+                    )
 
-        def difference(c, pair):
+        def add_turned(block, pair):
+            cols = slice(block * P, (block + 1) * P)
             if pair == 0:
-                diffs[c] = work.tile([P, 2, CHUNK, 2], F32, name="diff")
-            nc.vector.scalar_tensor_tensor(
-                diffs[c][:, pair, :, :].rearrange("p j e -> p (j e)"),
-                highs[c, pair][:].rearrange("p j e -> p (j e)"),
-                -0.5,
-                ups[c, pair][:].rearrange("p j e -> p (j e)"),
+                sums[block] = psum.tile([P, PACK, P], F32, name="sums", tag="bank2" if block == 3 else "bank6")
+            for t in (2 * pair, 2 * pair + 1):
+                for src, first in ((lower, True), (upper, False)):
+                    nc.tensor.matmul(
+                        sums[block][:, t, :], src[:, t, cols], ident[:], start=first, stop=not first, is_transpose=True
+                    )
+
+        def scale_round(block):
+            rows = work.tile([P, 2, P, 2], BF16, name="rows")
+            nc.vector.tensor_tensor(
+                rows[:],
+                sums[block][:].rearrange("j (u e) p -> j u p e", e=2),
+                gain[:].rearrange("j (p u e) -> j u p e", u=2, e=2),
                 ALU.mult,
-                ALU.add,
+            )
+            if block % 2 == 0:
+                turned[block // 2] = psum.tile([P, 2, 2, P], F32, name="turned", tag="bank7")
+            words = rows[:].rearrange("j u p e -> j (u p e)").bitcast(F32)
+            for u in range(2):
+                nc.tensor.transpose(turned[block // 2][:, block % 2, u, :], words[:, u * P : (u + 1) * P], ident[:])
+
+        def weave(half):
+            z[half] = work.tile([P, HALF * PACK], BF16, name="z", align_bytes=64)
+            nc.vector.tensor_copy(
+                out=z[half][:].bitcast(F32).rearrange("p (b j u) -> p b j u", b=2, u=2),
+                in_=turned[half][:].rearrange("p b u j -> p b j u"),
             )
 
-        def scale_round(c):
-            zs[c] = work.tile([P, CHUNK, 2, 2], BF16, name="z", align_bytes=64)
-            g = gain[:].rearrange("p (a e) -> p a e", e=2).unsqueeze(1).to_broadcast([P, CHUNK, 2, 2])
-            nc.vector.tensor_tensor(zs[c][:], diffs[c][:].rearrange("p a j e -> p j a e"), g, ALU.mult)
-
-        def second_product(c):
-            cols = slice(c * CHUNK, (c + 1) * CHUNK)
-            nc.vector.quantize_mx(
-                out=z_codes[:, cols].bitcast(FP8X4),
-                scales=z_plane[:, cols],
-                in_=zs[c][:].rearrange("p j a e -> p (j a e)"),
-            )
-            wide, first = divmod(c * CHUNK, WIDE)
+        def second_product(half):
+            cols = slice(half * HALF, (half + 1) * HALF)
+            nc.vector.quantize_mx(out=z_codes[:, cols].bitcast(FP8X4), scales=z_plane[:, cols], in_=z[half][:])
             for t in range(PACK):
-                if (wide, t // 2) not in h_bank:
-                    h_bank[wide, t // 2] = hbanks.tile([P, 2, WIDE], F32, name=f"h_bank{wide}{t // 2}")
+                if t % 2 == 0:
+                    tag = f"bank{4 - 4 * half + t // 2}"
+                    h_bank[half, t // 2] = psum.tile([P, 2, HALF], F32, name="h_bank", tag=tag)
                 nc.tensor.matmul_mx(
-                    out=h_bank[wide, t // 2][:, t % 2, first : first + CHUNK],
+                    out=h_bank[half, t // 2][:, t % 2, :],
                     lhsT=w2_codes[:, t, :].bitcast(FP4X4),
                     lhsT_scale=w2_plane[:, t, :],
                     rhs=z_codes[:, cols].bitcast(FP8X4),
@@ -198,103 +222,150 @@ def tile_picked_skipjointbgmid_none_po_kernel(
                     stop=True,
                 )
 
-        def fetch_ends(wide, pair):
-            tile = ring.tile([P, 2, 2 * WIDE], F32, name="ends")
-            ends[wide, pair] = tile
-            entries = slice(wide * WIDE // 16, (wide + 1) * WIDE // 16)
-            for e in range(2):
-                for side, places in enumerate((n2_sb, n3_sb)):
-                    nc.scalar.activation(
-                        tile[:, side, e * WIDE : (e + 1) * WIDE],
-                        y_rows[2 * pair + e][:].indirect(places[:, entries]),
-                        ACT.Copy,
-                    )
+        low_ends = keep.tile([P, 2, S], F32, name="low_ends")
+        high_ends = keep.tile([P, 2, HALF], F32, name="high_ends")
+        left_subtrahend = keep.tile([P, PACK, HALF], F32, name="left_subtrahend")
+        gate = keep.tile([P, PACK, S], F32, name="gate")
+        result = keep.tile([P, PACK, S], F32, name="result")
+        rounded = keep.tile([P, S, PACK], BF16, name="rounded", align_bytes=64)
 
-        def subtract(wide, pair, cols=slice(0, 2 * WIDE)):
-            tile = ends[wide, pair]
-            nc.vector.tensor_tensor(tile[:, 0, cols], tile[:, 0, cols], tile[:, 1, cols], ALU.subtract)
+        def within(cols):
+            return slice(cols.start % HALF, (cols.stop - 1) % HALF + 1)
 
-        def gate(wide, pair, cols=slice(0, 2 * WIDE)):
-            if (wide, pair) not in gates:
-                gates[wide, pair] = keep.tile([P, 2 * WIDE], F32, name=f"gate{wide}{pair}")
-            nc.scalar.activation(gates[wide, pair][:, cols], ends[wide, pair][:, 0, cols], ACT.Tanh)
+        def in_pair(ts):
+            return slice(ts.start % 2, (ts.stop - 1) % 2 + 1)
 
-        def multiply(wide, pair, cols=slice(0, 2 * WIDE)):
-            if wide not in results:
-                results[wide] = work.tile([P, 2, 2 * WIDE], F32, name="result")
-            res = results[wide]
-            nc.vector.tensor_tensor(
-                res[:, pair, cols],
-                h_bank[wide, pair][:].rearrange("p e j -> p (e j)")[:, cols],
-                gates[wide, pair][:, cols],
-                ALU.mult,
+        def homes(half, ts):
+            if half == 0:
+                first = low_ends[:, ts, 0:HALF] if ts.start < 2 else high_ends[:, in_pair(ts), :]
+                return first, left_subtrahend[:, ts, :]
+            if ts.start < 2:
+                return low_ends[:, ts, HALF:S], low_ends[:, ts, 0:HALF]
+            if ts.start == 2:
+                return high_ends[:, 0:1, :], high_ends[:, 1:2, :]
+            return low_ends[:, 0:1, HALF:S], low_ends[:, 1:2, HALF:S]
+
+        def fetch_end(side, half, t):
+            entries = slice(half * HALF // 16, (half + 1) * HALF // 16)
+            home = homes(half, slice(t, t + 1))[side]
+            places = (n2_sb, n3_sb)[side]
+            nc.scalar.activation(home[:, 0, :], y_rows[t][:].indirect(places[:, entries]), ACT.Copy)
+
+        def fetch_whole_minuend(t):
+            nc.scalar.activation(low_ends[:, t, :], y_rows[t][:].indirect(n2_sb[:]), ACT.Copy)
+
+        def fetch_minuend(half, t):
+            fetch_end(0, half, t)
+
+        def fetch_subtrahend(half, t):
+            fetch_end(1, half, t)
+
+        def subtract(ts, cols):
+            a, b = homes(cols.start // HALF, ts)
+            nc.vector.tensor_tensor(a[:, :, within(cols)], a[:, :, within(cols)], b[:, :, within(cols)], ALU.subtract)
+
+        def squash(ts, cols):
+            a = homes(cols.start // HALF, ts)[0]
+            nc.scalar.activation(gate[:, ts, cols], a[:, :, within(cols)], ACT.Tanh, scale=-2.0)
+
+        def multiply(ts, cols):
+            own = h_bank[cols.start // HALF, ts.start // 2][:, in_pair(ts), within(cols)]
+            nc.vector.tensor_tensor(result[:, ts, cols], own, gate[:, ts, cols], ALU.mult)
+
+        def store(ts, cols):
+            nc.sync.dma_start(out=out_rows[:, ts, cols], in_=result[:, ts, cols])
+
+        def round_result(copy, cols):
+            copy(
+                rounded[:, cols, :].rearrange("p (c i) t -> p c t i", i=4),
+                result[:, :, cols].rearrange("p t (c i) -> p c t i", i=4),
             )
 
-        def store(wide, ts):
-            res = results[wide][:].rearrange("p a (e j) -> p (a e) j", e=2)
-            nc.sync.dma_start(out=out_rows[:, ts, wide * WIDE : (wide + 1) * WIDE], in_=res[:, ts, :])
-
-        def round_result(wide):
-            roundeds[wide] = work.tile([P, WIDE, PACK], BF16, name="rounded", align_bytes=64)
-            nc.vector.tensor_copy(
-                out=roundeds[wide][:].rearrange("p (c i) t -> p c t i", i=4),
-                in_=results[wide][:].rearrange("p a (e c i) -> p c (a e) i", e=2, i=4),
-            )
-
-        def planes(wide):
-            cols = slice(wide * WIDE, (wide + 1) * WIDE)
+        def quantise_result(cols):
             nc.vector.quantize_mx(
                 out=o_codes[:, cols].bitcast(FP8X4),
                 scales=o_plane[:, cols],
-                in_=roundeds[wide][:].rearrange("p j t -> p (j t)"),
+                in_=rounded[:, cols, :].rearrange("p j t -> p (j t)"),
             )
+
+        def store_words(cols):
             nc.sync.dma_start(out=out_words[:, cols], in_=o_codes[:, cols])
 
-        deal_words(w2_codes)
+        for pair in range(2):
+            fetch_members(0, pair)
+            extremes(0, pair)
+            add_turned(0, pair)
+        w2_codes = keep.tile([P, PACK, 2 * P], U8, name="w2_codes", tag="members01", align_bytes=64)
+        deal_words(w2_codes, w2_raw)
+        w2_plane = keep.tile([P, PACK, P], U8, name="w2_plane", tag="members00", align_bytes=64)
         deal_scales(nc.vector, w2_plane, slice(0, 4))
-        units = [(c, pair) for c in range(CHUNKS) for pair in range(2)]
-        for k, (c, pair) in enumerate(units):
-            fetch_members(c, pair)
-            pair_low(c, pair)
-            if k > 0:
-                difference(*units[k - 1])
-            if pair == 1 and c > 0:
-                second_product(c - 1)
-            extremes(c, pair)
-            if pair == 0 and c > 0:
-                scale_round(c - 1)
+        fetch_members(1, 0)
+        scale_round(0)
+        extremes(1, 0)
+        add_turned(1, 0)
+        fetch_members(1, 1)
+        extremes(1, 1)
+        add_turned(1, 1)
+        fetch_members(2, 0)
+        extremes(2, 0)
+        scale_round(1)
+        add_turned(2, 0)
+        add_turned(3, 0)
+        fetch_members(2, 1)
+        extremes(2, 1)
+        add_turned(2, 1)
+        add_turned(3, 1)
+        weave(0)
 
-        last = CHUNKS - 1
-        left, right = slice(0, WIDE), slice(WIDE, 2 * WIDE)
-        fetch_ends(0, 0)
-        fetch_ends(0, 1)
-        fetch_ends(1, 0)
-        subtract(0, 0)
-        gate(0, 0)
-        difference(last, 1)
-        subtract(0, 1)
-        scale_round(last)
-        fetch_ends(1, 1)
-        gate(0, 1)
-        subtract(1, 0)
-        second_product(last)
-        multiply(0, 0)
-        gate(1, 0)
-        multiply(0, 1)
-        store(0, slice(0, 4))
-        subtract(1, 1, left)
-        round_result(0)
-        subtract(1, 1, right)
-        gate(1, 1, left)
-        gate(1, 1, right)
-        multiply(1, 0)
-        store(1, slice(0, 2))
-        planes(0)
-        multiply(1, 1, left)
-        multiply(1, 1, right)
-        store(1, slice(2, 4))
-        round_result(1)
-        planes(1)
+        left, right = slice(0, HALF), slice(HALF, S)
+        third, fourth = slice(HALF, HALF + P), slice(HALF + P, S)
+        low, high, two, three = slice(0, 2), slice(2, 4), slice(2, 3), slice(3, 4)
+        for t in range(2):
+            fetch_whole_minuend(t)
+            fetch_subtrahend(0, t)
+        for t in range(2, PACK):
+            fetch_minuend(0, t)
+            fetch_subtrahend(0, t)
+        subtract(low, left)
+        second_product(0)
+        squash(low, left)
+        scale_round(2)
+        scale_round(3)
+        subtract(high, left)
+        fetch_subtrahend(1, 0)
+        fetch_subtrahend(1, 1)
+        squash(high, left)
+        multiply(low, left)
+        weave(1)
+        subtract(low, right)
+        multiply(high, left)
+        store(slice(0, PACK), left)
+        second_product(1)
+        fetch_minuend(1, 2)
+        fetch_subtrahend(1, 2)
+        squash(low, right)
+        round_result(nc.vector.tensor_copy, left)
+        fetch_minuend(1, 3)
+        fetch_subtrahend(1, 3)
+        subtract(two, right)
+        quantise_result(left)
+        store_words(left)
+        squash(two, right)
+        multiply(low, right)
+        store(low, right)
+        subtract(three, third)
+        subtract(three, fourth)
+        squash(three, third)
+        squash(three, fourth)
+        multiply(two, right)
+        multiply(three, third)
+        multiply(three, fourth)
+        store(high, right)
+        round_result(nc.vector.tensor_copy, third)
+        round_result(nc.scalar.copy, fourth)
+        quantise_result(third)
+        quantise_result(fourth)
+        store_words(right)
 
         for q in range(4):
             nc.scalar.dma_start(

from contextlib import ExitStack

import concourse.mybir as mybir
from concourse.masks import make_identity

K, T, S, N, H, W = 512, 2048, 512, 512, 512, 2048
FLOPS = 2 * K * H * S + 2 * H * N * S

F32 = mybir.dt.float32
BF16 = mybir.dt.bfloat16
I32 = mybir.dt.int32
U32 = mybir.dt.uint32
U16 = mybir.dt.uint16
U8 = mybir.dt.uint8
FP8X4 = mybir.dt.float8_e4m3fn_x4
FP4X4 = mybir.dt.float4_e2m1fn_x4
ALU = mybir.AluOpType
ACT = mybir.ActivationFunctionType

P = 128
PACK = 4
HALF = 256
CHUNKS = ((0, 128), (128, 192), (320, 192))
MEMBERS = 4
WINDOW = 1024


def tile_picked_skipjointbgmid_none_po_kernel(
    tc, x_words, x_scales, w1_words, w1_scales, gn, w2_words, w2_scales, offs, n1, n2, n3, out_0, out_1, out_2
):
    nc = tc.nc
    with ExitStack() as ctx:
        keep = ctx.enter_context(tc.tile_pool(name="keep", bufs=1))
        work = ctx.enter_context(tc.tile_pool(name="work", bufs=2))
        psum = ctx.enter_context(tc.psum_pool(name="psum", bufs=1))

        offs_sb = keep.tile([P, S // 16], U16, name="offs_sb")
        n1_sb = keep.tile([P, W // 16], U16, name="n1_sb")
        n2_sb = keep.tile([P, S // 16], U16, name="n2_sb")
        n3_sb = keep.tile([P, S // 16], U16, name="n3_sb")
        x_table = keep.tile([P, T], I32, name="x_table", tag="x_table", align_bytes=64)
        x_bytes = keep.tile([P, T], U8, name="x_bytes", tag="x_bytes", align_bytes=64)
        w_raw = keep.tile([P, 2 * H], U8, name="w_raw", align_bytes=64)
        ws_raw = keep.tile([P, H], U8, name="ws_raw", align_bytes=64)

        def load_scale_rows(queues, tile, rows):
            for q, queue in enumerate(queues):
                queue.dma_start(
                    out=tile[32 * q : 32 * q + 4, :].bitcast(I32), in_=rows[0, 4 * q : 4 * q + 4, :].bitcast(I32)
                )

        nc.gpsimd.memset(x_bytes[:].bitcast(I32), 0)
        nc.gpsimd.memset(ws_raw[:].bitcast(I32), 0)
        y_rows = [keep.tile([P, WINDOW], F32, name=f"y_rows{t}") for t in range(PACK)]
        for t in range(PACK):
            nc.vector.memset(y_rows[t][:, S:], 0.0)
        nc.sync.dma_start(out=offs_sb[:], in_=offs)
        nc.sync.dma_start(out=w_raw[:].bitcast(I32), in_=w1_words[0].bitcast(I32))
        load_scale_rows([nc.sync] * 4, x_bytes, x_scales)
        nc.sync.dma_start(out=x_table[:], in_=x_words[0].rearrange("p c r -> p (c r)").bitcast(I32))
        load_scale_rows([nc.sync, nc.sync, nc.sync, nc.gpsimd], ws_raw, w1_scales)
        ident = keep.tile([P, P], F32, name="ident")
        make_identity(nc, ident[:])
        nc.sync.dma_start(out=n1_sb[:], in_=n1)
        nc.sync.dma_start(out=n2_sb[:], in_=n2)
        nc.sync.dma_start(out=n3_sb[:], in_=n3)

        def deal_words(codes, raw):
            nc.vector.tensor_copy(
                out=codes[:].rearrange("p t (m b) -> p t m b", b=2),
                in_=raw[:].rearrange("p (m t b) -> p t m b", t=PACK, b=2),
            )

        def deal_scales(engine, plane, ts):
            engine.tensor_copy(out=plane[:, ts, :], in_=ws_raw[:].rearrange("p (m t) -> p t m", t=PACK)[:, ts, :])

        w1_codes = keep.tile([P, PACK, 2 * P], U8, name="w1_codes", align_bytes=64)
        w1_plane = keep.tile([P, PACK, P], U8, name="w1_plane", align_bytes=64)
        x_codes = keep.tile([P, S], U32, name="x_codes", align_bytes=64)
        x_plane = keep.tile([P, S], U8, name="x_plane", align_bytes=64)

        deal_words(w1_codes, w_raw)
        deal_scales(nc.gpsimd, w1_plane, slice(0, 2))
        deal_scales(nc.gpsimd, w1_plane, slice(2, 4))
        nc.vector.tensor_copy(out=x_plane[:], in_=x_bytes[:].indirect(offs_sb[:]))
        for half in range(2):
            nc.vector.tensor_copy(
                out=x_codes[:, half * HALF : (half + 1) * HALF],
                in_=x_table[:].bitcast(U32).indirect(offs_sb[:, half * HALF // 16 : (half + 1) * HALF // 16]),
            )

        w2_raw = keep.tile([P, 2 * N], U8, name="w2_raw", tag="x_table", align_bytes=64)
        nc.sync.dma_start(out=w2_raw[:].bitcast(I32), in_=w2_words[0].bitcast(I32))
        load_scale_rows([nc.sync] * 4, ws_raw, w2_scales)
        gain = keep.tile([P, H], F32, name="gain", tag="x_bytes", align_bytes=64)
        nc.sync.dma_start(out=gain[:], in_=gn.rearrange("i o -> (i o)").partition_broadcast(P))

        y_bank = {}

        def first_product(t, half):
            cols = slice(half * HALF, (half + 1) * HALF)
            if t % 2 == 0:
                y_bank[t // 2, half] = psum.tile([P, 2, HALF], F32, name="y_bank", tag=f"bank{2 * half + t // 2}")
            nc.tensor.matmul_mx(
                out=y_bank[t // 2, half][:, t % 2, :],
                lhsT=w1_codes[:, t, :].bitcast(FP4X4),
                lhsT_scale=w1_plane[:, t, :],
                rhs=x_codes[:, cols].bitcast(FP8X4),
                rhs_scale=x_plane[:, cols],
                start=True,
                stop=True,
            )

        def fill_window(t, half):
            cols = slice(half * HALF, (half + 1) * HALF)
            src = y_bank[t // 2, half][:, t % 2, :]
            if t == 0:
                nc.scalar.activation(y_rows[t][:, cols], src, ACT.Copy, scale=-0.5)
            else:
                nc.vector.tensor_scalar(y_rows[t][:, cols], src, -0.5, None, ALU.mult)

        first_product(0, 0)
        first_product(1, 0)
        fill_window(0, 0)
        first_product(0, 1)
        fill_window(0, 1)
        first_product(1, 1)
        for half in range(2):
            first_product(2, half)
            first_product(3, half)
        for t in range(1, PACK):
            for half in range(2):
                fill_window(t, half)

        z_codes = keep.tile([P, S], U32, name="z_codes", align_bytes=64)
        z_plane = keep.tile([P, S], U8, name="z_plane", align_bytes=64)
        o_codes = keep.tile([P, S], I32, name="o_codes", align_bytes=64)
        o_plane = keep.tile([P, S], U8, name="o_plane", align_bytes=64)
        out_rows = out_0.rearrange("(p t) j -> p t j", t=PACK)
        out_words = out_1[0].rearrange("p c r -> p (c r)").bitcast(I32)
        upper = keep.tile([P, PACK, S], F32, name="upper")
        lower = keep.tile([P, PACK, S], F32, name="lower")

        members, sums, turned, z, h_bank = ({} for k in range(5))

        def fetch_members(c, pair):
            first, width = CHUNKS[c]
            tile = keep.tile([P, 2, width * MEMBERS], F32, name="members", tag=f"members{c}{pair}", align_bytes=64)
            members[c, pair] = tile[:].rearrange("p e (j i) -> p (e j) i", i=MEMBERS)
            entries = slice(first * MEMBERS // 16, (first + width) * MEMBERS // 16)
            for e in range(2):
                nc.scalar.activation(tile[:, e, :], y_rows[2 * pair + e][:].indirect(n1_sb[:, entries]), ACT.Copy)

        def extremes(c, pair):
            m = members[c, pair]
            first, width = CHUNKS[c]
            ts = slice(2 * pair, 2 * pair + 2)
            hi = work.tile([P, 2, width, 2], F32, name="hi")
            lo = work.tile([P, 2, width, 2], F32, name="lo")
            nc.vector.tensor_tensor(hi[:].rearrange("p e j i -> p (e j) i"), m[:, :, 0:2], m[:, :, 2:4], ALU.max)
            nc.vector.tensor_tensor(lo[:].rearrange("p e j i -> p (e j) i"), m[:, :, 0:2], m[:, :, 2:4], ALU.min)
            top = work.tile([P, 2, width], F32, name="top")
            nc.vector.tensor_tensor(top[:], hi[:, :, :, 0], hi[:, :, :, 1], ALU.max)
            nc.vector.tensor_tensor(lower[:, ts, first : first + width], lo[:, :, :, 0], lo[:, :, :, 1], ALU.min)
            for half in range(2):
                a, b = max(first, half * HALF), min(first + width, (half + 1) * HALF)
                if a < b:
                    nc.vector.scalar_tensor_tensor(
                        upper[:, ts, a:b],
                        top[:, :, a - first : b - first],
                        -2.0,
                        y_bank[pair, half][:, :, a - half * HALF : b - half * HALF],
                        ALU.mult,
                        ALU.max,
                    )

        def add_turned(block, pair):
            cols = slice(block * P, (block + 1) * P)
            if pair == 0:
                sums[block] = psum.tile([P, PACK, P], F32, name="sums", tag="bank2" if block == 3 else "bank6")
            for t in (2 * pair, 2 * pair + 1):
                for src, first in ((lower, True), (upper, False)):
                    nc.tensor.matmul(
                        sums[block][:, t, :], src[:, t, cols], ident[:], start=first, stop=not first, is_transpose=True
                    )

        def scale_round(block):
            rows = work.tile([P, 2, P, 2], BF16, name="rows")
            nc.vector.tensor_tensor(
                rows[:],
                sums[block][:].rearrange("j (u e) p -> j u p e", e=2),
                gain[:].rearrange("j (p u e) -> j u p e", u=2, e=2),
                ALU.mult,
            )
            if block % 2 == 0:
                turned[block // 2] = psum.tile([P, 2, 2, P], F32, name="turned", tag="bank7")
            words = rows[:].rearrange("j u p e -> j (u p e)").bitcast(F32)
            for u in range(2):
                nc.tensor.transpose(turned[block // 2][:, block % 2, u, :], words[:, u * P : (u + 1) * P], ident[:])

        def weave(half):
            z[half] = work.tile([P, HALF * PACK], BF16, name="z", align_bytes=64)
            nc.vector.tensor_copy(
                out=z[half][:].bitcast(F32).rearrange("p (b j u) -> p b j u", b=2, u=2),
                in_=turned[half][:].rearrange("p b u j -> p b j u"),
            )

        def second_product(half):
            cols = slice(half * HALF, (half + 1) * HALF)
            nc.vector.quantize_mx(out=z_codes[:, cols].bitcast(FP8X4), scales=z_plane[:, cols], in_=z[half][:])
            for t in range(PACK):
                if t % 2 == 0:
                    tag = f"bank{4 - 4 * half + t // 2}"
                    h_bank[half, t // 2] = psum.tile([P, 2, HALF], F32, name="h_bank", tag=tag)
                nc.tensor.matmul_mx(
                    out=h_bank[half, t // 2][:, t % 2, :],
                    lhsT=w2_codes[:, t, :].bitcast(FP4X4),
                    lhsT_scale=w2_plane[:, t, :],
                    rhs=z_codes[:, cols].bitcast(FP8X4),
                    rhs_scale=z_plane[:, cols],
                    start=True,
                    stop=True,
                )

        low_ends = keep.tile([P, 2, S], F32, name="low_ends")
        high_ends = keep.tile([P, 2, HALF], F32, name="high_ends")
        left_subtrahend = keep.tile([P, PACK, HALF], F32, name="left_subtrahend")
        gate = keep.tile([P, PACK, S], F32, name="gate")
        result = keep.tile([P, PACK, S], F32, name="result")
        rounded = keep.tile([P, S, PACK], BF16, name="rounded", align_bytes=64)

        def within(cols):
            return slice(cols.start % HALF, (cols.stop - 1) % HALF + 1)

        def in_pair(ts):
            return slice(ts.start % 2, (ts.stop - 1) % 2 + 1)

        def homes(half, ts):
            if half == 0:
                first = low_ends[:, ts, 0:HALF] if ts.start < 2 else high_ends[:, in_pair(ts), :]
                return first, left_subtrahend[:, ts, :]
            if ts.start < 2:
                return low_ends[:, ts, HALF:S], low_ends[:, ts, 0:HALF]
            if ts.start == 2:
                return high_ends[:, 0:1, :], high_ends[:, 1:2, :]
            return low_ends[:, 0:1, HALF:S], low_ends[:, 1:2, HALF:S]

        def fetch_end(side, half, t):
            entries = slice(half * HALF // 16, (half + 1) * HALF // 16)
            home = homes(half, slice(t, t + 1))[side]
            places = (n2_sb, n3_sb)[side]
            nc.scalar.activation(home[:, 0, :], y_rows[t][:].indirect(places[:, entries]), ACT.Copy)

        def fetch_whole_minuend(t):
            nc.scalar.activation(low_ends[:, t, :], y_rows[t][:].indirect(n2_sb[:]), ACT.Copy)

        def fetch_minuend(half, t):
            fetch_end(0, half, t)

        def fetch_subtrahend(half, t):
            fetch_end(1, half, t)

        def subtract(ts, cols):
            a, b = homes(cols.start // HALF, ts)
            nc.vector.tensor_tensor(a[:, :, within(cols)], a[:, :, within(cols)], b[:, :, within(cols)], ALU.subtract)

        def squash(ts, cols):
            a = homes(cols.start // HALF, ts)[0]
            nc.scalar.activation(gate[:, ts, cols], a[:, :, within(cols)], ACT.Tanh, scale=-2.0)

        def multiply(ts, cols):
            own = h_bank[cols.start // HALF, ts.start // 2][:, in_pair(ts), within(cols)]
            nc.vector.tensor_tensor(result[:, ts, cols], own, gate[:, ts, cols], ALU.mult)

        def store(ts, cols):
            nc.sync.dma_start(out=out_rows[:, ts, cols], in_=result[:, ts, cols])

        def round_result(copy, cols):
            copy(
                rounded[:, cols, :].rearrange("p (c i) t -> p c t i", i=4),
                result[:, :, cols].rearrange("p t (c i) -> p c t i", i=4),
            )

        def quantise_result(cols):
            nc.vector.quantize_mx(
                out=o_codes[:, cols].bitcast(FP8X4),
                scales=o_plane[:, cols],
                in_=rounded[:, cols, :].rearrange("p j t -> p (j t)"),
            )

        def store_words(cols):
            nc.sync.dma_start(out=out_words[:, cols], in_=o_codes[:, cols])

        for pair in range(2):
            fetch_members(0, pair)
            extremes(0, pair)
            add_turned(0, pair)
        w2_codes = keep.tile([P, PACK, 2 * P], U8, name="w2_codes", tag="members01", align_bytes=64)
        deal_words(w2_codes, w2_raw)
        w2_plane = keep.tile([P, PACK, P], U8, name="w2_plane", tag="members00", align_bytes=64)
        deal_scales(nc.vector, w2_plane, slice(0, 4))
        fetch_members(1, 0)
        scale_round(0)
        extremes(1, 0)
        add_turned(1, 0)
        fetch_members(1, 1)
        extremes(1, 1)
        add_turned(1, 1)
        fetch_members(2, 0)
        extremes(2, 0)
        scale_round(1)
        add_turned(2, 0)
        add_turned(3, 0)
        fetch_members(2, 1)
        extremes(2, 1)
        add_turned(2, 1)
        add_turned(3, 1)
        weave(0)

        left, right = slice(0, HALF), slice(HALF, S)
        third, fourth = slice(HALF, HALF + P), slice(HALF + P, S)
        low, high, two, three = slice(0, 2), slice(2, 4), slice(2, 3), slice(3, 4)
        for t in range(2):
            fetch_whole_minuend(t)
            fetch_subtrahend(0, t)
        for t in range(2, PACK):
            fetch_minuend(0, t)
            fetch_subtrahend(0, t)
        subtract(low, left)
        second_product(0)
        squash(low, left)
        scale_round(2)
        scale_round(3)
        subtract(high, left)
        fetch_subtrahend(1, 0)
        fetch_subtrahend(1, 1)
        squash(high, left)
        multiply(low, left)
        weave(1)
        subtract(low, right)
        multiply(high, left)
        store(slice(0, PACK), left)
        second_product(1)
        fetch_minuend(1, 2)
        fetch_subtrahend(1, 2)
        squash(low, right)
        round_result(nc.vector.tensor_copy, left)
        fetch_minuend(1, 3)
        fetch_subtrahend(1, 3)
        subtract(two, right)
        quantise_result(left)
        store_words(left)
        squash(two, right)
        multiply(low, right)
        store(low, right)
        subtract(three, third)
        subtract(three, fourth)
        squash(three, third)
        squash(three, fourth)
        multiply(two, right)
        multiply(three, third)
        multiply(three, fourth)
        store(high, right)
        round_result(nc.vector.tensor_copy, third)
        round_result(nc.scalar.copy, fourth)
        quantise_result(third)
        quantise_result(fourth)
        store_words(right)

        for q in range(4):
            nc.scalar.dma_start(
                out=out_2[0, 4 * q : 4 * q + 4, :].bitcast(I32), in_=o_plane[32 * q : 32 * q + 4, :].bitcast(I32)
            )
